import numpy as np
import ml_dtypes


def mxq(x, axis, fmt="e4m3"):
    dtype, down = {"e4m3": (ml_dtypes.float8_e4m3fn, 7), "e5m2": (ml_dtypes.float8_e5m2, 14)}[fmt]
    v = np.moveaxis(np.asarray(x, np.float32).astype(ml_dtypes.bfloat16).astype(np.float64), axis, -1)
    blocks = v.reshape(v.shape[:-1] + (-1, 32))
    amax = np.abs(blocks).max(-1, keepdims=True)
    byte = np.maximum(np.where(amax > 0, np.frexp(amax)[1] - 1 + 127, 0) - down, 1)
    scale = np.exp2(byte - 127.0)
    codes = (blocks / scale).astype(np.float32).astype(dtype).astype(np.float64)
    return np.moveaxis((codes * scale).reshape(v.shape), -1, axis)


WIDE = False


def mx_kscale(k):
    if not WIDE:
        return np.ones(k)
    levels = np.array([10, -10, 5, -5, 0])
    if k % 512:
        return np.exp2(np.random.permutation(np.resize(levels, k // 32))).repeat(32)
    a = np.empty((k // 512, 16))
    for p in range(k // 512):
        a[p, :8] = np.random.permutation(np.resize(levels, 8))
        for g in range(8):
            far = levels[np.abs(levels - a[p, g]) >= 10]
            a[p, g + 8] = far[np.random.randint(len(far))]
    return np.exp2(a.ravel()).repeat(32)


def f64(x):
    return np.asarray(x).astype(np.float64)


def striped8(idx):
    return np.concatenate([x.reshape(-1, 16).T for x in idx]).astype(np.uint16)


def runs(offs, k):
    lists = np.stack([offs[16 * r : 16 * r + 16].T.reshape(-1) for r in range(8)]).astype(np.int64)
    return lists[np.arange(k) % 512 // 64]


def pack_weight(w):
    k, n = w.shape
    w = f64(np.asarray(w, np.float32).astype(ml_dtypes.bfloat16)).reshape(k // 32, 32, n)
    amax = np.abs(w).max(1)
    byte = np.clip(np.where(amax > 0, np.frexp(amax)[1] - 1 + 127 - 7, 1), 1, 254)
    scaled = (w * np.exp2(127.0 - byte)[:, None, :]).reshape(k, n).astype(np.float32)
    words = np.ascontiguousarray(scaled.reshape(k // 512, 128, 4, n).transpose(0, 1, 3, 2)).astype(ml_dtypes.float8_e4m3fn).view(np.uint8)
    return words, np.ascontiguousarray(byte.astype(np.uint8).reshape(k // 512, 16, n))


def unpack_weight(words, scales):
    g, p, n, _ = words.shape
    vals = np.ascontiguousarray(words).view(ml_dtypes.float8_e4m3fn).astype(np.float64) * np.repeat(np.exp2(scales.astype(np.float64) - 127.0), 8, axis=1)[..., None]
    return vals.transpose(0, 1, 3, 2).reshape(g * 512, n)


def sigmoid(v):
    return 1.0 / (1.0 + np.exp(-np.maximum(v, -700.0)))

def planes(y):
    n, m = y.shape
    v = y.astype(np.float32).astype(ml_dtypes.bfloat16).astype(np.float64).reshape(n // 32, 32, m)
    top = np.abs(v).max(1)
    byte = np.clip(np.where(top > 0, np.frexp(top)[1] - 1 + 127 - 7, 1), 1, 254)
    codes = (v * np.exp2(127.0 - byte)[:, None, :]).reshape(n, m).astype(np.float32).astype(ml_dtypes.float8_e4m3fn).view(np.uint8)
    words = codes.reshape(n // 512, 128, 4, m).transpose(0, 1, 3, 2)
    return np.ascontiguousarray(words), np.ascontiguousarray(byte.astype(np.uint8).reshape(n // 512, 16, m))


K, T, S, N = 512, 2048, 512, 512


def setup_inputs():
    n = np.random.standard_normal
    s = mx_kscale(K)[:, None]
    packed_xT = pack_weight(n((K, T)) * s)
    return {
        "x_words": packed_xT[0],
        "x_scales": packed_xT[1],
        "w1": (n((K, N)) / np.sqrt(3 * K) / s).astype(np.float32),
        "w2": (n((K, N)) / np.sqrt(3 * K) / s).astype(np.float32),
        "w3": (n((K, N)) / np.sqrt(3 * K) / s).astype(np.float32),
        "w4": (n((K, N)) / np.sqrt(3 * K) / s).astype(np.float32),
        "w5": (n((K, N)) / np.sqrt(3 * K) / s).astype(np.float32),
        "w6": (n((K, N)) / np.sqrt(3 * K) / s).astype(np.float32),
        "offs": striped8(np.stack([np.random.permutation(T)[:S] for _ in range(8)])),
        "tap1": striped8(np.stack([np.random.permutation(T)[:S] for _ in range(8)])),
        "tap2": striped8(np.stack([np.random.permutation(T)[:S] for _ in range(8)])),
    }


def reference(x_words, x_scales, w1, w2, w3, w4, w5, w6, offs, tap1, tap2):
    xq = unpack_weight(x_words, x_scales)[np.arange(K)[:, None], runs(offs, K)]
    x_tap1 = unpack_weight(x_words, x_scales)[np.arange(K)[:, None], runs(tap1, K)]
    x_tap2 = unpack_weight(x_words, x_scales)[np.arange(K)[:, None], runs(tap2, K)]
    o = mxq(f64(w1), 0, "e4m3").T @ xq + mxq(f64(w2), 0, "e4m3").T @ x_tap1 + mxq(f64(w3), 0, "e4m3").T @ x_tap2
    s = sigmoid(mxq(f64(w4), 0, "e4m3").T @ xq + mxq(f64(w5), 0, "e4m3").T @ x_tap1 + mxq(f64(w6), 0, "e4m3").T @ x_tap2)
    out_0 = o * s
    return (out_0,) + planes(out_0)

@@ -1,0 +1,181 @@
+from contextlib import ExitStack
+
+import concourse.mybir as mybir
+
+K, T, S, N = 512, 2048, 512, 512
+FLOPS = 2 * 6 * K * N * S
+
+F32 = mybir.dt.float32
+BF16 = mybir.dt.bfloat16
+I32 = mybir.dt.int32
+U32 = mybir.dt.uint32
+U16 = mybir.dt.uint16
+U8 = mybir.dt.uint8
+FP8X4 = mybir.dt.float8_e4m3fn_x4
+SIGMOID = mybir.ActivationFunctionType.Sigmoid
+MULT = mybir.AluOpType.mult
+
+P = 128
+PACK = 4
+TAPS = 3
+SHIFT = 14
+MOVED_ROWS = 112
+
+
+def tile_picked_gdconv_none_po_kernel(
+    tc, x_words, x_scales, w1, w2, w3, w4, w5, w6, offs, tap1, tap2, out_0, out_1, out_2
+):
+    nc = tc.nc
+    with ExitStack() as ctx:
+        keep = ctx.enter_context(tc.tile_pool(name="keep", bufs=1))
+        psum = ctx.enter_context(tc.psum_pool(name="psum", bufs=1))
+
+        scale_table = keep.tile([P, T], U8, name="scale_table", align_bytes=64)
+        nc.vector.memset(scale_table[:].bitcast(I32), 0)
+        x_scale = keep.tile([P, TAPS * S], U8, name="x_scale", align_bytes=64)
+        nc.gpsimd.memset(x_scale[:].bitcast(I32), 0)
+        warm = keep.tile([P, 2], F32, name="warm")
+        nc.vector.memset(warm[:, 0:1], 0.0)
+        nc.scalar.activation(warm[:, 1:2], warm[:, 0:1], SIGMOID)
+
+        lists = []
+        for i, src in enumerate((offs, tap1, tap2)):
+            lst = keep.tile([P, S // 16], U16, name="list%d" % i)
+            nc.sync.dma_start(lst[:], src)
+            lists.append(lst)
+        for q in range(4):
+            p0 = 32 * q + SHIFT
+            nc.scalar.dma_start(
+                scale_table[p0 : p0 + 4, :].bitcast(I32), x_scales[0, 4 * q : 4 * q + 4, :].bitcast(I32)
+            )
+
+        def load_weight(name, w, c0, c1):
+            raw = keep.tile([P, PACK, c1 - c0], F32, name=name)
+            nc.sync.dma_start(raw[:], w.rearrange("(p j) c -> p j c", j=PACK)[:, :, c0:c1])
+            return raw
+
+        word_table = keep.tile([P, T], I32, name="word_table", align_bytes=64)
+        nc.sync.dma_start(word_table[:], x_words[0].rearrange("p c r -> p (c r)").bitcast(I32))
+        weights = (w1, w2, w3, w4, w5, w6)
+        raws = {}
+        for i in (3, 4, 5, 0, 1, 2):
+            for h in range(2):
+                raws[i, h] = load_weight("raw%d_%d" % (i, h), weights[i], 256 * h, 256 * (h + 1))
+
+        grouped = [keep.tile([P, PACK, P, PACK], BF16, name="grouped%d" % i, align_bytes=64) for i in range(6)]
+        codes = [keep.tile([P, N], U32, name="codes%d" % i, align_bytes=64) for i in range(6)]
+        scales = [keep.tile([P, N], U8, name="scales%d" % i, align_bytes=64) for i in range(6)]
+
+        def cast(engine, i, h):
+            raw = raws[i, h]
+            dst = grouped[i][:, :, 64 * h : 64 * (h + 1), :].rearrange("p t m j -> p m j t")
+            src = raw[:].rearrange("p j (m t) -> p m j t", t=PACK)
+            if engine == "scalar":
+                nc.scalar.copy(dst, src)
+            else:
+                nc.vector.tensor_copy(dst, src)
+
+        def quantize(i, t0, t1):
+            nc.vector.quantize_mx(
+                out=codes[i][:, t0 * P : t1 * P].bitcast(FP8X4),
+                scales=scales[i][:, t0 * P : t1 * P],
+                in_=grouped[i][:, t0:t1].rearrange("p t m j -> p (t m j)"),
+            )
+
+        picked_scale = keep.tile([P, TAPS * S], U8, name="picked_scale", align_bytes=64)
+        x_codes = [keep.tile([P, S], U32, name="x_codes%d" % i, align_bytes=64) for i in range(TAPS)]
+
+        def gather_words(i):
+            nc.vector.tensor_copy(x_codes[i][:], word_table[:].bitcast(U32).indirect(lists[i][:]))
+
+        gather_words(0)
+        gather_words(1)
+        for i in range(TAPS):
+            nc.vector.tensor_copy(picked_scale[:, i * S : (i + 1) * S], scale_table[:].indirect(lists[i][:]))
+        gather_words(2)
+        for i in (3, 4):
+            for h in range(2):
+                cast("scalar", i, h)
+        nc.scalar.dma_start(
+            x_scale[0:MOVED_ROWS, :].bitcast(I32), picked_scale[SHIFT : SHIFT + MOVED_ROWS, :].bitcast(I32)
+        )
+
+        banks = [psum.tile([P, S], F32, name="bank%d" % b) for b in range(8)]
+
+        def multiply(i, t):
+            tap = i % TAPS
+            nc.tensor.matmul_mx(
+                out=banks[(i // TAPS) * PACK + t][:],
+                lhsT=codes[i][:, t * P : (t + 1) * P].bitcast(FP8X4),
+                lhsT_scale=scales[i][:, t * P : (t + 1) * P],
+                rhs=x_codes[tap][:].bitcast(FP8X4),
+                rhs_scale=x_scale[:, tap * S : (tap + 1) * S],
+                start=(tap == 0),
+                stop=(tap == TAPS - 1),
+            )
+
+        quantize(3, 0, 4)
+        for t in range(PACK):
+            multiply(3, t)
+        quantize(4, 0, 4)
+        for t in range(PACK):
+            multiply(4, t)
+        cast("scalar", 5, 0)
+        cast("vector", 5, 1)
+        quantize(5, 0, 4)
+        gate = keep.tile([P, PACK, S], F32, name="gate")
+        for t in range(PACK):
+            multiply(5, t)
+        cast("scalar", 0, 0)
+        cast("vector", 0, 1)
+        for t in range(PACK):
+            nc.scalar.activation(gate[:, t, :], banks[PACK + t][:], SIGMOID)
+        quantize(0, 0, 4)
+        for t in range(PACK):
+            multiply(0, t)
+        cast("vector", 1, 0)
+        cast("vector", 1, 1)
+        quantize(1, 0, 4)
+        for t in range(PACK):
+            multiply(1, t)
+        cast("scalar", 2, 0)
+        cast("vector", 2, 1)
+        for t in range(PACK):
+            quantize(2, t, t + 1)
+            multiply(2, t)
+
+        H = S // 2
+        y_words = keep.tile([P, S], U32, name="y_words", align_bytes=64)
+        y_scales = keep.tile([P, S], U8, name="y_scales", align_bytes=64)
+        out_rows = out_0.rearrange("(p t) j -> p t j", t=PACK)
+        words_out = out_1[0].rearrange("p c r -> p (c r)").bitcast(I32)
+        ys, rounded = [], []
+        for h in range(2):
+            cols = slice(h * H, (h + 1) * H)
+            y = keep.tile([P, PACK, H], F32, name="y%d" % h)
+            for t in range(PACK):
+                nc.vector.tensor_tensor(y[:, t, :], banks[t][:, cols], gate[:, t, cols], MULT)
+            nc.sync.dma_start(out_rows[:, :, cols], y[:])
+            ys.append(y)
+        for h in range(2):
+            yb = keep.tile([P, H, PACK], BF16, name="yb%d" % h, align_bytes=64)
+            dst = yb[:].rearrange("p (c i) t -> p c t i", i=PACK)
+            src = ys[h][:].rearrange("p t (c i) -> p c t i", i=PACK)
+            if h == 0:
+                nc.scalar.copy(dst, src)
+            else:
+                nc.vector.tensor_copy(dst, src)
+            rounded.append(yb)
+        for h in range(2):
+            cols = slice(h * H, (h + 1) * H)
+            nc.vector.quantize_mx(
+                out=y_words[:, cols].bitcast(FP8X4),
+                scales=y_scales[:, cols],
+                in_=rounded[h][:].rearrange("p j t -> p (j t)"),
+            )
+            nc.sync.dma_start(words_out[:, cols], y_words[:, cols].bitcast(I32))
+        for q in range(4):
+            eng = nc.scalar if q % 2 else nc.sync
+            eng.dma_start(
+                out_2[0, 4 * q : 4 * q + 4, :].bitcast(I32), y_scales[32 * q : 32 * q + 4, :].bitcast(I32)
+            )

@@ -20,6 +20,7 @@ PACK = 4
 TAPS = 3
 SHIFT = 14
 MOVED_ROWS = 112
+RING = 6
 
 
 def tile_picked_gdconv_none_po_kernel(
@@ -28,10 +29,11 @@ def tile_picked_gdconv_none_po_kernel(
     nc = tc.nc
     with ExitStack() as ctx:
         keep = ctx.enter_context(tc.tile_pool(name="keep", bufs=1))
+        ring = ctx.enter_context(tc.tile_pool(name="ring", bufs=RING))
         psum = ctx.enter_context(tc.psum_pool(name="psum", bufs=1))
 
         scale_table = keep.tile([P, T], U8, name="scale_table", align_bytes=64)
-        nc.vector.memset(scale_table[:].bitcast(I32), 0)
+        nc.gpsimd.memset(scale_table[:].bitcast(I32), 0)
         x_scale = keep.tile([P, TAPS * S], U8, name="x_scale", align_bytes=64)
         nc.gpsimd.memset(x_scale[:].bitcast(I32), 0)
         warm = keep.tile([P, 2], F32, name="warm")
@@ -43,24 +45,28 @@ def tile_picked_gdconv_none_po_kernel(
             lst = keep.tile([P, S // 16], U16, name="list%d" % i)
             nc.sync.dma_start(lst[:], src)
             lists.append(lst)
+
+        weights = (w1, w2, w3, w4, w5, w6)
+        halves = [(i, h) for i in (3, 4, 5, 0, 1, 2) for h in range(2)]
+        raws = {}
+
+        def load_half(n):
+            i, h = halves[n]
+            raw = ring.tile([P, PACK, 256], F32, name="raw")
+            nc.sync.dma_start(raw[:], weights[i].rearrange("(p j) c -> p j c", j=PACK)[:, :, 256 * h : 256 * (h + 1)])
+            raws[i, h] = raw
+
+        load_half(0)
         for q in range(4):
             p0 = 32 * q + SHIFT
-            nc.scalar.dma_start(
+            nc.sync.dma_start(
                 scale_table[p0 : p0 + 4, :].bitcast(I32), x_scales[0, 4 * q : 4 * q + 4, :].bitcast(I32)
             )
-
-        def load_weight(name, w, c0, c1):
-            raw = keep.tile([P, PACK, c1 - c0], F32, name=name)
-            nc.sync.dma_start(raw[:], w.rearrange("(p j) c -> p j c", j=PACK)[:, :, c0:c1])
-            return raw
-
+        load_half(1)
         word_table = keep.tile([P, T], I32, name="word_table", align_bytes=64)
         nc.sync.dma_start(word_table[:], x_words[0].rearrange("p c r -> p (c r)").bitcast(I32))
-        weights = (w1, w2, w3, w4, w5, w6)
-        raws = {}
-        for i in (3, 4, 5, 0, 1, 2):
-            for h in range(2):
-                raws[i, h] = load_weight("raw%d_%d" % (i, h), weights[i], 256 * h, 256 * (h + 1))
+        for n in range(2, RING):
+            load_half(n)
 
         grouped = [keep.tile([P, PACK, P, PACK], BF16, name="grouped%d" % i, align_bytes=64) for i in range(6)]
         codes = [keep.tile([P, N], U32, name="codes%d" % i, align_bytes=64) for i in range(6)]
@@ -74,6 +80,9 @@ def tile_picked_gdconv_none_po_kernel(
                 nc.scalar.copy(dst, src)
             else:
                 nc.vector.tensor_copy(dst, src)
+            n = halves.index((i, h)) + RING
+            if n < len(halves):
+                load_half(n)
 
         def quantize(i, t0, t1):
             nc.vector.quantize_mx(
@@ -88,17 +97,17 @@ def tile_picked_gdconv_none_po_kernel(
         def gather_words(i):
             nc.vector.tensor_copy(x_codes[i][:], word_table[:].bitcast(U32).indirect(lists[i][:]))
 
-        gather_words(0)
-        gather_words(1)
         for i in range(TAPS):
             nc.vector.tensor_copy(picked_scale[:, i * S : (i + 1) * S], scale_table[:].indirect(lists[i][:]))
-        gather_words(2)
-        for i in (3, 4):
-            for h in range(2):
-                cast("scalar", i, h)
+        cast("scalar", 3, 0)
+        cast("scalar", 3, 1)
         nc.scalar.dma_start(
             x_scale[0:MOVED_ROWS, :].bitcast(I32), picked_scale[SHIFT : SHIFT + MOVED_ROWS, :].bitcast(I32)
         )
+        for i in range(TAPS):
+            gather_words(i)
+        cast("scalar", 4, 0)
+        cast("scalar", 4, 1)
 
         banks = [psum.tile([P, S], F32, name="bank%d" % b) for b in range(8)]
 

@@ -20,7 +20,7 @@ PACK = 4
 TAPS = 3
 SHIFT = 14
 MOVED_ROWS = 112
-RING = 6
+RING = 3
 
 
 def tile_picked_gdconv_none_po_kernel(
@@ -32,57 +32,51 @@ def tile_picked_gdconv_none_po_kernel(
         ring = ctx.enter_context(tc.tile_pool(name="ring", bufs=RING))
         psum = ctx.enter_context(tc.psum_pool(name="psum", bufs=1))
 
-        scale_table = keep.tile([P, T], U8, name="scale_table", align_bytes=64)
-        nc.gpsimd.memset(scale_table[:].bitcast(I32), 0)
+        scale_table = keep.tile([P, T], U8, name="scale_table", tag="table_then_w4_scales", align_bytes=64)
+        nc.gpsimd.memset(scale_table[:, : T // 2].bitcast(I32), 0)
+        nc.vector.memset(scale_table[:, T // 2 :].bitcast(I32), 0)
         x_scale = keep.tile([P, TAPS * S], U8, name="x_scale", align_bytes=64)
         nc.gpsimd.memset(x_scale[:].bitcast(I32), 0)
         warm = keep.tile([P, 2], F32, name="warm")
         nc.vector.memset(warm[:, 0:1], 0.0)
         nc.scalar.activation(warm[:, 1:2], warm[:, 0:1], SIGMOID)
 
-        lists = []
-        for i, src in enumerate((offs, tap1, tap2)):
-            lst = keep.tile([P, S // 16], U16, name="list%d" % i)
-            nc.sync.dma_start(lst[:], src)
-            lists.append(lst)
-
+        lists = [keep.tile([P, S // 16], U16, name="list%d" % i) for i in range(TAPS)]
         weights = (w1, w2, w3, w4, w5, w6)
-        halves = [(i, h) for i in (3, 4, 5, 0, 1, 2) for h in range(2)]
         raws = {}
 
-        def load_half(n):
-            i, h = halves[n]
-            raw = ring.tile([P, PACK, 256], F32, name="raw")
-            nc.sync.dma_start(raw[:], weights[i].rearrange("(p j) c -> p j c", j=PACK)[:, :, 256 * h : 256 * (h + 1)])
-            raws[i, h] = raw
+        def load(i):
+            raw = ring.tile([P, PACK, N], F32, name="raw")
+            nc.sync.dma_start(raw[:], weights[i].rearrange("(p j) c -> p j c", j=PACK))
+            raws[i] = raw
 
-        load_half(0)
+        for lst, src in zip(lists, (offs, tap1, tap2)):
+            nc.sync.dma_start(lst[:], src)
+        raws.setdefault(3, ring.tile([P, PACK, N], F32, name="raw"))
+        w4_rows = w4.rearrange("(p j) c -> p j c", j=PACK)
+        nc.sync.dma_start(raws[3][:, 0:2, :], w4_rows[:, 0:2, :])
         for q in range(4):
             p0 = 32 * q + SHIFT
             nc.sync.dma_start(
                 scale_table[p0 : p0 + 4, :].bitcast(I32), x_scales[0, 4 * q : 4 * q + 4, :].bitcast(I32)
             )
-        load_half(1)
-        word_table = keep.tile([P, T], I32, name="word_table", align_bytes=64)
+        nc.sync.dma_start(raws[3][:, 2:4, :], w4_rows[:, 2:4, :])
+        load(4)
+        word_table = keep.tile([P, T], I32, name="word_table", tag="table_then_w5_scales", align_bytes=64)
         nc.sync.dma_start(word_table[:], x_words[0].rearrange("p c r -> p (c r)").bitcast(I32))
-        for n in range(2, RING):
-            load_half(n)
+        load(5)
 
         grouped = [keep.tile([P, PACK, P, PACK], BF16, name="grouped%d" % i, align_bytes=64) for i in range(6)]
         codes = [keep.tile([P, N], U32, name="codes%d" % i, align_bytes=64) for i in range(6)]
-        scales = [keep.tile([P, N], U8, name="scales%d" % i, align_bytes=64) for i in range(6)]
+        scales = {i: keep.tile([P, N], U8, name="scales%d" % i, align_bytes=64) for i in (0, 1, 2, 5)}
 
-        def cast(engine, i, h):
-            raw = raws[i, h]
-            dst = grouped[i][:, :, 64 * h : 64 * (h + 1), :].rearrange("p t m j -> p m j t")
-            src = raw[:].rearrange("p j (m t) -> p m j t", t=PACK)
+        def cast(engine, i, m0, m1):
+            dst = grouped[i][:, :, m0:m1, :].rearrange("p t m j -> p m j t")
+            src = raws[i][:, :, PACK * m0 : PACK * m1].rearrange("p j (m t) -> p m j t", t=PACK)
             if engine == "scalar":
                 nc.scalar.copy(dst, src)
             else:
                 nc.vector.tensor_copy(dst, src)
-            n = halves.index((i, h)) + RING
-            if n < len(halves):
-                load_half(n)
 
         def quantize(i, t0, t1):
             nc.vector.quantize_mx(
@@ -99,15 +93,18 @@ def tile_picked_gdconv_none_po_kernel(
 
         for i in range(TAPS):
             nc.vector.tensor_copy(picked_scale[:, i * S : (i + 1) * S], scale_table[:].indirect(lists[i][:]))
-        cast("scalar", 3, 0)
-        cast("scalar", 3, 1)
-        nc.scalar.dma_start(
+        scales.setdefault(3, keep.tile([P, N], U8, name="scales3", tag="table_then_w4_scales", align_bytes=64))
+        cast("scalar", 3, 0, 128)
+        nc.sync.dma_start(
             x_scale[0:MOVED_ROWS, :].bitcast(I32), picked_scale[SHIFT : SHIFT + MOVED_ROWS, :].bitcast(I32)
         )
+        load(0)
+        cast("scalar", 4, 0, 128)
+        load(1)
+        quantize(3, 0, 4)
         for i in range(TAPS):
             gather_words(i)
-        cast("scalar", 4, 0)
-        cast("scalar", 4, 1)
+        scales.setdefault(4, keep.tile([P, N], U8, name="scales4", tag="table_then_w5_scales", align_bytes=64))
 
         banks = [psum.tile([P, S], F32, name="bank%d" % b) for b in range(8)]
 
@@ -123,32 +120,30 @@ def tile_picked_gdconv_none_po_kernel(
                 stop=(tap == TAPS - 1),
             )
 
-        quantize(3, 0, 4)
         for t in range(PACK):
             multiply(3, t)
         quantize(4, 0, 4)
         for t in range(PACK):
             multiply(4, t)
-        cast("scalar", 5, 0)
-        cast("vector", 5, 1)
+        cast("scalar", 5, 0, 128)
+        load(2)
         quantize(5, 0, 4)
         gate = keep.tile([P, PACK, S], F32, name="gate")
         for t in range(PACK):
             multiply(5, t)
-        cast("scalar", 0, 0)
-        cast("vector", 0, 1)
+        cast("scalar", 0, 0, 64)
+        cast("vector", 0, 64, 128)
         for t in range(PACK):
             nc.scalar.activation(gate[:, t, :], banks[PACK + t][:], SIGMOID)
         quantize(0, 0, 4)
         for t in range(PACK):
             multiply(0, t)
-        cast("vector", 1, 0)
-        cast("vector", 1, 1)
+        cast("vector", 1, 0, 128)
         quantize(1, 0, 4)
         for t in range(PACK):
             multiply(1, t)
-        cast("scalar", 2, 0)
-        cast("vector", 2, 1)
+        cast("scalar", 2, 0, 44)
+        cast("vector", 2, 44, 128)
         for t in range(PACK):
             quantize(2, t, t + 1)
             multiply(2, t)
@@ -157,32 +152,29 @@ def tile_picked_gdconv_none_po_kernel(
         y_words = keep.tile([P, S], U32, name="y_words", align_bytes=64)
         y_scales = keep.tile([P, S], U8, name="y_scales", align_bytes=64)
         out_rows = out_0.rearrange("(p t) j -> p t j", t=PACK)
-        words_out = out_1[0].rearrange("p c r -> p (c r)").bitcast(I32)
-        ys, rounded = [], []
+        y = keep.tile([P, PACK, S], F32, name="y")
+        yb = keep.tile([P, S, PACK], BF16, name="yb", align_bytes=64)
+
+        def gate_product(t, c0, c1):
+            nc.vector.tensor_tensor(y[:, t, c0:c1], banks[t][:, c0:c1], gate[:, t, c0:c1], MULT)
+
+        for t in range(2):
+            gate_product(t, 0, S)
+            nc.sync.dma_start(out_rows[:, t, :], y[:, t, :])
         for h in range(2):
-            cols = slice(h * H, (h + 1) * H)
-            y = keep.tile([P, PACK, H], F32, name="y%d" % h)
-            for t in range(PACK):
-                nc.vector.tensor_tensor(y[:, t, :], banks[t][:, cols], gate[:, t, cols], MULT)
-            nc.sync.dma_start(out_rows[:, :, cols], y[:])
-            ys.append(y)
-        for h in range(2):
-            yb = keep.tile([P, H, PACK], BF16, name="yb%d" % h, align_bytes=64)
-            dst = yb[:].rearrange("p (c i) t -> p c t i", i=PACK)
-            src = ys[h][:].rearrange("p t (c i) -> p c t i", i=PACK)
+            for t in range(2, PACK):
+                gate_product(t, h * H, (h + 1) * H)
+            dst = yb[:, h * H : (h + 1) * H, :].rearrange("p (c i) t -> p c t i", i=PACK)
+            src = y[:, :, h * H : (h + 1) * H].rearrange("p t (c i) -> p c t i", i=PACK)
             if h == 0:
                 nc.scalar.copy(dst, src)
             else:
+                nc.sync.dma_start(out_rows[:, 2:PACK, :], y[:, 2:PACK, :])
                 nc.vector.tensor_copy(dst, src)
-            rounded.append(yb)
-        for h in range(2):
-            cols = slice(h * H, (h + 1) * H)
-            nc.vector.quantize_mx(
-                out=y_words[:, cols].bitcast(FP8X4),
-                scales=y_scales[:, cols],
-                in_=rounded[h][:].rearrange("p j t -> p (j t)"),
-            )
-            nc.sync.dma_start(words_out[:, cols], y_words[:, cols].bitcast(I32))
+        nc.vector.quantize_mx(
+            out=y_words[:].bitcast(FP8X4), scales=y_scales[:], in_=yb[:].rearrange("p j t -> p (j t)")
+        )
+        nc.sync.dma_start(out_1[0].rearrange("p c r -> p (c r)").bitcast(I32), y_words[:].bitcast(I32))
         for q in range(4):
             eng = nc.scalar if q % 2 else nc.sync
             eng.dma_start(

@@ -21,6 +21,7 @@ TAPS = 3
 SHIFT = 14
 MOVED_ROWS = 112
 RING = 3
+Y_SPLIT = 88
 
 
 def tile_picked_gdconv_none_po_kernel(
@@ -152,29 +153,33 @@ def tile_picked_gdconv_none_po_kernel(
         y_words = keep.tile([P, S], U32, name="y_words", align_bytes=64)
         y_scales = keep.tile([P, S], U8, name="y_scales", align_bytes=64)
         out_rows = out_0.rearrange("(p t) j -> p t j", t=PACK)
-        y = keep.tile([P, PACK, S], F32, name="y")
-        yb = keep.tile([P, S, PACK], BF16, name="yb", align_bytes=64)
+        words_out = out_1[0].rearrange("p c r -> p (c r)").bitcast(I32)
+        y = [keep.tile([P, PACK, H], F32, name="y%d" % h) for h in range(2)]
+        yb = [keep.tile([P, H, PACK], BF16, name="yb%d" % h, align_bytes=64) for h in range(2)]
 
-        def gate_product(t, c0, c1):
-            nc.vector.tensor_tensor(y[:, t, c0:c1], banks[t][:, c0:c1], gate[:, t, c0:c1], MULT)
+        def views(h, c0, c1):
+            dst = yb[h][:, c0:c1, :].rearrange("p (c i) t -> p c t i", i=PACK)
+            return dst, y[h][:, :, c0:c1].rearrange("p t (c i) -> p c t i", i=PACK)
 
-        for t in range(2):
-            gate_product(t, 0, S)
-            nc.sync.dma_start(out_rows[:, t, :], y[:, t, :])
+        def quantize_y(h):
+            cols = slice(h * H, (h + 1) * H)
+            nc.vector.quantize_mx(
+                out=y_words[:, cols].bitcast(FP8X4), scales=y_scales[:, cols], in_=yb[h][:].rearrange("p j t -> p (j t)")
+            )
+            nc.sync.dma_start(words_out[:, cols], y_words[:, cols].bitcast(I32))
+
         for h in range(2):
-            for t in range(2, PACK):
-                gate_product(t, h * H, (h + 1) * H)
-            dst = yb[:, h * H : (h + 1) * H, :].rearrange("p (c i) t -> p c t i", i=PACK)
-            src = y[:, :, h * H : (h + 1) * H].rearrange("p t (c i) -> p c t i", i=PACK)
+            cols = slice(h * H, (h + 1) * H)
+            for t in range(PACK):
+                nc.vector.tensor_tensor(y[h][:, t, :], banks[t][:, cols], gate[:, t, cols], MULT)
+                if t % 2:
+                    nc.sync.dma_start(out_rows[:, t - 1 : t + 1, cols], y[h][:, t - 1 : t + 1, :])
             if h == 0:
-                nc.scalar.copy(dst, src)
-            else:
-                nc.sync.dma_start(out_rows[:, 2:PACK, :], y[:, 2:PACK, :])
-                nc.vector.tensor_copy(dst, src)
-        nc.vector.quantize_mx(
-            out=y_words[:].bitcast(FP8X4), scales=y_scales[:], in_=yb[:].rearrange("p j t -> p (j t)")
-        )
-        nc.sync.dma_start(out_1[0].rearrange("p c r -> p (c r)").bitcast(I32), y_words[:].bitcast(I32))
+                nc.scalar.copy(*views(0, 0, H))
+        nc.scalar.copy(*views(1, 0, Y_SPLIT))
+        nc.vector.tensor_copy(*views(1, Y_SPLIT, H))
+        quantize_y(0)
+        quantize_y(1)
         for q in range(4):
             eng = nc.scalar if q % 2 else nc.sync
             eng.dma_start(

@@ -18,9 +18,8 @@ MULT = mybir.AluOpType.mult
 P = 128
 PACK = 4
 TAPS = 3
-SHIFT = 14
-MOVED_ROWS = 112
-RING = 3
+RING = 2
+X_FIRST = 512
 Y_SPLIT = 88
 
 
@@ -33,7 +32,9 @@ def tile_picked_gdconv_none_po_kernel(
         ring = ctx.enter_context(tc.tile_pool(name="ring", bufs=RING))
         psum = ctx.enter_context(tc.psum_pool(name="psum", bufs=1))
 
-        scale_table = keep.tile([P, T], U8, name="scale_table", tag="table_then_w4_scales", align_bytes=64)
+        head = ctx.enter_context(tc.tile_pool(name="head", bufs=1))
+        RAW = PACK * N * 4
+        scale_table = head.tile([P, T], U8, name="scale_table", offset=RAW - T // 2, align_bytes=64)
         nc.gpsimd.memset(scale_table[:, : T // 2].bitcast(I32), 0)
         nc.vector.memset(scale_table[:, T // 2 :].bitcast(I32), 0)
         x_scale = keep.tile([P, TAPS * S], U8, name="x_scale", align_bytes=64)
@@ -46,38 +47,35 @@ def tile_picked_gdconv_none_po_kernel(
         weights = (w1, w2, w3, w4, w5, w6)
         raws = {}
 
-        def load(i):
-            raw = ring.tile([P, PACK, N], F32, name="raw")
+        def load(i, raw):
             nc.sync.dma_start(raw[:], weights[i].rearrange("(p j) c -> p j c", j=PACK))
             raws[i] = raw
 
-        for lst, src in zip(lists, (offs, tap1, tap2)):
-            nc.sync.dma_start(lst[:], src)
-        raws.setdefault(3, ring.tile([P, PACK, N], F32, name="raw"))
-        w4_rows = w4.rearrange("(p j) c -> p j c", j=PACK)
-        nc.sync.dma_start(raws[3][:, 0:2, :], w4_rows[:, 0:2, :])
-        for q in range(4):
-            p0 = 32 * q + SHIFT
-            nc.sync.dma_start(
-                scale_table[p0 : p0 + 4, :].bitcast(I32), x_scales[0, 4 * q : 4 * q + 4, :].bitcast(I32)
-            )
-        nc.sync.dma_start(raws[3][:, 2:4, :], w4_rows[:, 2:4, :])
-        load(4)
-        word_table = keep.tile([P, T], I32, name="word_table", tag="table_then_w5_scales", align_bytes=64)
-        nc.sync.dma_start(word_table[:], x_words[0].rearrange("p c r -> p (c r)").bitcast(I32))
-        load(5)
+        nc.sync.dma_start(lists[0][:], offs)
+        word_table = keep.tile([P, T], I32, name="word_table", align_bytes=64)
+        x_rows = x_words[0].rearrange("p c r -> p (c r)").bitcast(I32)
+        nc.sync.dma_start(word_table[:, :X_FIRST], x_rows[:, :X_FIRST])
+        nc.sync.dma_start(scale_table[0:P:8, :].bitcast(I32), x_scales[0].bitcast(I32))
+        nc.sync.dma_start(lists[1][:], tap1)
+        nc.sync.dma_start(lists[2][:], tap2)
+        nc.sync.dma_start(word_table[:, X_FIRST:], x_rows[:, X_FIRST:])
+        load(3, ring.tile([P, PACK, N], F32, name="raw"))
+        load(4, ring.tile([P, PACK, N], F32, name="raw"))
 
         grouped = [keep.tile([P, PACK, P, PACK], BF16, name="grouped%d" % i, align_bytes=64) for i in range(6)]
         codes = [keep.tile([P, N], U32, name="codes%d" % i, align_bytes=64) for i in range(6)]
-        scales = {i: keep.tile([P, N], U8, name="scales%d" % i, align_bytes=64) for i in (0, 1, 2, 5)}
+        scales = [keep.tile([P, N], U8, name="scales%d" % i, align_bytes=64) for i in range(6)]
 
-        def cast(engine, i, m0, m1):
-            dst = grouped[i][:, :, m0:m1, :].rearrange("p t m j -> p m j t")
-            src = raws[i][:, :, PACK * m0 : PACK * m1].rearrange("p j (m t) -> p m j t", t=PACK)
-            if engine == "scalar":
-                nc.scalar.copy(dst, src)
-            else:
-                nc.vector.tensor_copy(dst, src)
+        def cast(i, split, first=0, last=P):
+            for engine, m0, m1 in (("scalar", first, split), ("vector", split, last)):
+                if m0 == m1:
+                    continue
+                dst = grouped[i][:, :, m0:m1, :].rearrange("p t m j -> p m j t")
+                src = raws[i][:, :, PACK * m0 : PACK * m1].rearrange("p j (m t) -> p m j t", t=PACK)
+                if engine == "scalar":
+                    nc.scalar.copy(dst, src)
+                else:
+                    nc.vector.tensor_copy(dst, src)
 
         def quantize(i, t0, t1):
             nc.vector.quantize_mx(
@@ -89,23 +87,16 @@ def tile_picked_gdconv_none_po_kernel(
         picked_scale = keep.tile([P, TAPS * S], U8, name="picked_scale", align_bytes=64)
         x_codes = [keep.tile([P, S], U32, name="x_codes%d" % i, align_bytes=64) for i in range(TAPS)]
 
-        def gather_words(i):
-            nc.vector.tensor_copy(x_codes[i][:], word_table[:].bitcast(U32).indirect(lists[i][:]))
-
         for i in range(TAPS):
             nc.vector.tensor_copy(picked_scale[:, i * S : (i + 1) * S], scale_table[:].indirect(lists[i][:]))
-        scales.setdefault(3, keep.tile([P, N], U8, name="scales3", tag="table_then_w4_scales", align_bytes=64))
-        cast("scalar", 3, 0, 128)
-        nc.sync.dma_start(
-            x_scale[0:MOVED_ROWS, :].bitcast(I32), picked_scale[SHIFT : SHIFT + MOVED_ROWS, :].bitcast(I32)
-        )
-        load(0)
-        cast("scalar", 4, 0, 128)
-        load(1)
-        quantize(3, 0, 4)
+        for q in range(4):
+            nc.sync.dma_start(
+                x_scale[32 * q : 32 * q + 4, :].bitcast(I32), picked_scale[32 * q : 32 * q + 32 : 8, :].bitcast(I32)
+            )
+        load(5, head.tile([P, PACK, N], F32, name="raw_w6", offset=0))
+        load(0, head.tile([P, PACK, N], F32, name="raw_w1", offset=RAW))
         for i in range(TAPS):
-            gather_words(i)
-        scales.setdefault(4, keep.tile([P, N], U8, name="scales4", tag="table_then_w5_scales", align_bytes=64))
+            nc.vector.tensor_copy(x_codes[i][:], word_table[:].bitcast(U32).indirect(lists[i][:]))
 
         banks = [psum.tile([P, S], F32, name="bank%d" % b) for b in range(8)]
 
@@ -121,32 +112,41 @@ def tile_picked_gdconv_none_po_kernel(
                 stop=(tap == TAPS - 1),
             )
 
-        for t in range(PACK):
-            multiply(3, t)
-        quantize(4, 0, 4)
-        for t in range(PACK):
-            multiply(4, t)
-        cast("scalar", 5, 0, 128)
-        load(2)
-        quantize(5, 0, 4)
+        def stage(i, split):
+            cast(i, split)
+            quantize(i, 0, 4)
+            for t in range(PACK):
+                multiply(i, t)
+
+        stage(3, 128)
+        load(1, ring.tile([P, PACK, N], F32, name="raw"))
+        stage(4, 128)
+        raws[2] = ring.tile([P, PACK, N], F32, name="raw")
+        w3_rows = w3.rearrange("(p j) c -> p j c", j=PACK)
+        for c0 in (0, N // 2):
+            nc.sync.dma_start(raws[2][:, :, c0 : c0 + N // 2], w3_rows[:, :, c0 : c0 + N // 2])
+        stage(5, 96)
+        stage(0, 64)
         gate = keep.tile([P, PACK, S], F32, name="gate")
         for t in range(PACK):
-            multiply(5, t)
-        cast("scalar", 0, 0, 64)
-        cast("vector", 0, 64, 128)
-        for t in range(PACK):
             nc.scalar.activation(gate[:, t, :], banks[PACK + t][:], SIGMOID)
-        quantize(0, 0, 4)
+        stage(1, 0)
+        half = P // 2
+
+        def quantize_half(t, m0):
+            cols = slice(t * P + m0, t * P + m0 + half)
+            nc.vector.quantize_mx(
+                out=codes[2][:, cols].bitcast(FP8X4),
+                scales=scales[2][:, cols],
+                in_=grouped[2][:, t, m0 : m0 + half].rearrange("p m j -> p (m j)"),
+            )
+
+        cast(2, half, 0, half)
         for t in range(PACK):
-            multiply(0, t)
-        cast("vector", 1, 0, 128)
-        quantize(1, 0, 4)
+            quantize_half(t, 0)
+        cast(2, half + 20, half, P)
         for t in range(PACK):
-            multiply(1, t)
-        cast("scalar", 2, 0, 44)
-        cast("vector", 2, 44, 128)
-        for t in range(PACK):
-            quantize(2, t, t + 1)
+            quantize_half(t, half)
             multiply(2, t)
 
         H = S // 2

@@ -18,8 +18,6 @@ MULT = mybir.AluOpType.mult
 P = 128
 PACK = 4
 TAPS = 3
-RING = 2
-X_FIRST = 512
 Y_SPLIT = 88
 
 
@@ -29,12 +27,9 @@ def tile_picked_gdconv_none_po_kernel(
     nc = tc.nc
     with ExitStack() as ctx:
         keep = ctx.enter_context(tc.tile_pool(name="keep", bufs=1))
-        ring = ctx.enter_context(tc.tile_pool(name="ring", bufs=RING))
         psum = ctx.enter_context(tc.psum_pool(name="psum", bufs=1))
 
-        head = ctx.enter_context(tc.tile_pool(name="head", bufs=1))
-        RAW = PACK * N * 4
-        scale_table = head.tile([P, T], U8, name="scale_table", offset=RAW - T // 2, align_bytes=64)
+        scale_table = keep.tile([P, T], U8, name="scale_table", tag="scale_table_then_w6", align_bytes=64)
         nc.gpsimd.memset(scale_table[:, : T // 2].bitcast(I32), 0)
         nc.vector.memset(scale_table[:, T // 2 :].bitcast(I32), 0)
         x_scale = keep.tile([P, TAPS * S], U8, name="x_scale", align_bytes=64)
@@ -47,22 +42,28 @@ def tile_picked_gdconv_none_po_kernel(
         weights = (w1, w2, w3, w4, w5, w6)
         raws = {}
 
-        def load(i, raw):
-            nc.sync.dma_start(raw[:], weights[i].rearrange("(p j) c -> p j c", j=PACK))
-            raws[i] = raw
+        def load(i, tag, m0=0, m1=P):
+            raw = keep.tile([P, PACK, PACK * (m1 - m0)], F32, name="raw%d_%d" % (i, m0), tag=tag, align_bytes=64)
+            rows = weights[i].rearrange("(p j) c -> p j c", j=PACK)
+            nc.sync.dma_start(raw[:], rows[:, :, PACK * m0 : PACK * m1])
+            raws.setdefault(i, []).append((m0, m1, raw))
 
-        nc.sync.dma_start(lists[0][:], offs)
         word_table = keep.tile([P, T], I32, name="word_table", align_bytes=64)
         x_rows = x_words[0].rearrange("p c r -> p (c r)").bitcast(I32)
-        nc.sync.dma_start(word_table[:, :X_FIRST], x_rows[:, :X_FIRST])
+        nc.sync.dma_start(lists[0][:], offs)
+        nc.sync.dma_start(word_table[:, : T // 4], x_rows[:, : T // 4])
         nc.sync.dma_start(scale_table[0:P:8, :].bitcast(I32), x_scales[0].bitcast(I32))
         nc.sync.dma_start(lists[1][:], tap1)
         nc.sync.dma_start(lists[2][:], tap2)
-        nc.sync.dma_start(word_table[:, X_FIRST:], x_rows[:, X_FIRST:])
-        load(3, ring.tile([P, PACK, N], F32, name="raw"))
-        load(4, ring.tile([P, PACK, N], F32, name="raw"))
+        load(3, "w4_then_w1")
+        nc.sync.dma_start(word_table[:, T // 4 :], x_rows[:, T // 4 :])
+        load(4, "w5_then_w3")
+        load(5, "w6_first_half", 0, P // 2)
 
-        grouped = [keep.tile([P, PACK, P, PACK], BF16, name="grouped%d" % i, align_bytes=64) for i in range(6)]
+        grouped = [
+            keep.tile([P, PACK, P, PACK], BF16, name="grouped%d" % i, tag="grouped%d" % i, align_bytes=64)
+            for i in range(6)
+        ]
         codes = [keep.tile([P, N], U32, name="codes%d" % i, align_bytes=64) for i in range(6)]
         scales = [keep.tile([P, N], U8, name="scales%d" % i, align_bytes=64) for i in range(6)]
 
@@ -71,7 +72,8 @@ def tile_picked_gdconv_none_po_kernel(
                 if m0 == m1:
                     continue
                 dst = grouped[i][:, :, m0:m1, :].rearrange("p t m j -> p m j t")
-                src = raws[i][:, :, PACK * m0 : PACK * m1].rearrange("p j (m t) -> p m j t", t=PACK)
+                base, raw = [(a, r) for a, b, r in raws[i] if a <= m0 and m1 <= b][0]
+                src = raw[:, :, PACK * (m0 - base) : PACK * (m1 - base)].rearrange("p j (m t) -> p m j t", t=PACK)
                 if engine == "scalar":
                     nc.scalar.copy(dst, src)
                 else:
@@ -93,9 +95,12 @@ def tile_picked_gdconv_none_po_kernel(
             nc.sync.dma_start(
                 x_scale[32 * q : 32 * q + 4, :].bitcast(I32), picked_scale[32 * q : 32 * q + 32 : 8, :].bitcast(I32)
             )
-        load(5, head.tile([P, PACK, N], F32, name="raw_w6", offset=0))
-        load(0, head.tile([P, PACK, N], F32, name="raw_w1", offset=RAW))
+        load(5, "scale_table_then_w6", P // 2, P)
+        cast(3, 128)
+        load(0, "w4_then_w1")
         for i in range(TAPS):
+            if i == 1:
+                quantize(3, 0, 4)
             nc.vector.tensor_copy(x_codes[i][:], word_table[:].bitcast(U32).indirect(lists[i][:]))
 
         banks = [psum.tile([P, S], F32, name="bank%d" % b) for b in range(8)]
@@ -118,35 +123,26 @@ def tile_picked_gdconv_none_po_kernel(
             for t in range(PACK):
                 multiply(i, t)
 
-        stage(3, 128)
-        load(1, ring.tile([P, PACK, N], F32, name="raw"))
+        load(1, "grouped3")
+        for t in range(PACK):
+            multiply(3, t)
         stage(4, 128)
-        raws[2] = ring.tile([P, PACK, N], F32, name="raw")
-        w3_rows = w3.rearrange("(p j) c -> p j c", j=PACK)
-        for c0 in (0, N // 2):
-            nc.sync.dma_start(raws[2][:, :, c0 : c0 + N // 2], w3_rows[:, :, c0 : c0 + N // 2])
-        stage(5, 96)
-        stage(0, 64)
-        gate = keep.tile([P, PACK, S], F32, name="gate")
+        load(2, "w5_then_w3", 0, P // 2)
+        load(2, "grouped4", P // 2, P)
+        cast(5, 64, 0, 64)
+        cast(5, 96, 64, 128)
+        quantize(5, 0, 4)
+        for t in range(PACK):
+            multiply(5, t)
+        stage(0, 48)
+        gate = keep.tile([P, PACK, S], F32, name="gate", tag="w4_then_w1", align_bytes=64)
         for t in range(PACK):
             nc.scalar.activation(gate[:, t, :], banks[PACK + t][:], SIGMOID)
         stage(1, 0)
-        half = P // 2
-
-        def quantize_half(t, m0):
-            cols = slice(t * P + m0, t * P + m0 + half)
-            nc.vector.quantize_mx(
-                out=codes[2][:, cols].bitcast(FP8X4),
-                scales=scales[2][:, cols],
-                in_=grouped[2][:, t, m0 : m0 + half].rearrange("p m j -> p (m j)"),
-            )
-
-        cast(2, half, 0, half)
+        cast(2, 64, 0, 64)
+        cast(2, 84, 64, 128)
         for t in range(PACK):
-            quantize_half(t, 0)
-        cast(2, half + 20, half, P)
-        for t in range(PACK):
-            quantize_half(t, half)
+            quantize(2, t, t + 1)
             multiply(2, t)
 
         H = S // 2

@@ -129,23 +129,26 @@ def tile_picked_gdconv_none_po_kernel(
         stage(4, 128)
         load(2, "w5_then_w3", 0, P // 2)
         load(2, "grouped4", P // 2, P)
-        cast(5, 64, 0, 64)
-        cast(5, 96, 64, 128)
-        quantize(5, 0, 4)
-        for t in range(PACK):
-            multiply(5, t)
+        stage(5, 64)
         stage(0, 48)
-        gate = keep.tile([P, PACK, S], F32, name="gate", tag="w4_then_w1", align_bytes=64)
-        for t in range(PACK):
-            nc.scalar.activation(gate[:, t, :], banks[PACK + t][:], SIGMOID)
-        stage(1, 0)
-        cast(2, 64, 0, 64)
+        H = S // 2
+        gate_tags = ("w4_then_w1", "grouped4")
+        gate = []
+
+        def sigmoids(h):
+            gate.append(keep.tile([P, PACK, H], F32, name="gate%d" % h, tag=gate_tags[h], align_bytes=64))
+            for t in range(PACK):
+                nc.scalar.activation(gate[h][:, t, :], banks[PACK + t][:, h * H : (h + 1) * H], SIGMOID)
+
+        sigmoids(0)
+        stage(1, 36)
+        cast(2, 48, 0, 64)
         cast(2, 84, 64, 128)
         for t in range(PACK):
             quantize(2, t, t + 1)
             multiply(2, t)
+        sigmoids(1)
 
-        H = S // 2
         y_words = keep.tile([P, S], U32, name="y_words", align_bytes=64)
         y_scales = keep.tile([P, S], U8, name="y_scales", align_bytes=64)
         out_rows = out_0.rearrange("(p t) j -> p t j", t=PACK)
@@ -167,7 +170,7 @@ def tile_picked_gdconv_none_po_kernel(
         for h in range(2):
             cols = slice(h * H, (h + 1) * H)
             for t in range(PACK):
-                nc.vector.tensor_tensor(y[h][:, t, :], banks[t][:, cols], gate[:, t, cols], MULT)
+                nc.vector.tensor_tensor(y[h][:, t, :], banks[t][:, cols], gate[h][:, t, :], MULT)
                 if t % 2:
                     nc.sync.dma_start(out_rows[:, t - 1 : t + 1, cols], y[h][:, t - 1 : t + 1, :])
             if h == 0:

@@ -29,7 +29,7 @@ def tile_picked_gdconv_none_po_kernel(
         keep = ctx.enter_context(tc.tile_pool(name="keep", bufs=1))
         psum = ctx.enter_context(tc.psum_pool(name="psum", bufs=1))
 
-        scale_table = keep.tile([P, T], U8, name="scale_table", tag="scale_table_then_w6", align_bytes=64)
+        scale_table = keep.tile([P, T], U8, name="scale_table", tag="scale_table_then_w1", align_bytes=64)
         nc.gpsimd.memset(scale_table[:, : T // 2].bitcast(I32), 0)
         nc.vector.memset(scale_table[:, T // 2 :].bitcast(I32), 0)
         x_scale = keep.tile([P, TAPS * S], U8, name="x_scale", align_bytes=64)
@@ -50,15 +50,14 @@ def tile_picked_gdconv_none_po_kernel(
 
         word_table = keep.tile([P, T], I32, name="word_table", align_bytes=64)
         x_rows = x_words[0].rearrange("p c r -> p (c r)").bitcast(I32)
-        nc.sync.dma_start(lists[0][:], offs)
-        nc.sync.dma_start(word_table[:, : T // 4], x_rows[:, : T // 4])
+        nc.sync.dma_start(word_table[:, : T // 2], x_rows[:, : T // 2])
+        for lst, src in zip(lists, (offs, tap1, tap2)):
+            nc.sync.dma_start(lst[:], src)
         nc.sync.dma_start(scale_table[0:P:8, :].bitcast(I32), x_scales[0].bitcast(I32))
-        nc.sync.dma_start(lists[1][:], tap1)
-        nc.sync.dma_start(lists[2][:], tap2)
-        load(3, "w4_then_w1")
-        nc.sync.dma_start(word_table[:, T // 4 :], x_rows[:, T // 4 :])
+        load(3, "w4_then_w2")
+        nc.sync.dma_start(word_table[:, T // 2 :], x_rows[:, T // 2 :])
         load(4, "w5_then_w3")
-        load(5, "w6_first_half", 0, P // 2)
+        load(5, "w6")
 
         grouped = [
             keep.tile([P, PACK, P, PACK], BF16, name="grouped%d" % i, tag="grouped%d" % i, align_bytes=64)
@@ -87,7 +86,8 @@ def tile_picked_gdconv_none_po_kernel(
             )
 
         picked_scale = keep.tile([P, TAPS * S], U8, name="picked_scale", align_bytes=64)
-        x_codes = [keep.tile([P, S], U32, name="x_codes%d" % i, align_bytes=64) for i in range(TAPS)]
+        x_tags = ("x_codes0", "x_codes1", "grouped3")
+        x_codes = [keep.tile([P, S], U32, name="x_codes%d" % i, tag=x_tags[i], align_bytes=64) for i in range(TAPS)]
 
         for i in range(TAPS):
             nc.vector.tensor_copy(picked_scale[:, i * S : (i + 1) * S], scale_table[:].indirect(lists[i][:]))
@@ -95,11 +95,11 @@ def tile_picked_gdconv_none_po_kernel(
             nc.sync.dma_start(
                 x_scale[32 * q : 32 * q + 4, :].bitcast(I32), picked_scale[32 * q : 32 * q + 32 : 8, :].bitcast(I32)
             )
-        load(5, "scale_table_then_w6", P // 2, P)
+        load(0, "scale_table_then_w1")
         cast(3, 128)
-        load(0, "w4_then_w1")
+        load(1, "w4_then_w2")
         for i in range(TAPS):
-            if i == 1:
+            if i == 2:
                 quantize(3, 0, 4)
             nc.vector.tensor_copy(x_codes[i][:], word_table[:].bitcast(U32).indirect(lists[i][:]))
 
@@ -123,16 +123,14 @@ def tile_picked_gdconv_none_po_kernel(
             for t in range(PACK):
                 multiply(i, t)
 
-        load(1, "grouped3")
         for t in range(PACK):
             multiply(3, t)
         stage(4, 128)
-        load(2, "w5_then_w3", 0, P // 2)
-        load(2, "grouped4", P // 2, P)
+        load(2, "w5_then_w3")
         stage(5, 64)
-        stage(0, 48)
+        stage(0, 72)
         H = S // 2
-        gate_tags = ("w4_then_w1", "grouped4")
+        gate_tags = ("scale_table_then_w1", "w5_then_w3")
         gate = []
 
         def sigmoids(h):
@@ -141,9 +139,14 @@ def tile_picked_gdconv_none_po_kernel(
                 nc.scalar.activation(gate[h][:, t, :], banks[PACK + t][:, h * H : (h + 1) * H], SIGMOID)
 
         sigmoids(0)
-        stage(1, 36)
-        cast(2, 48, 0, 64)
-        cast(2, 84, 64, 128)
+        stage(1, 0)
+        for u, split in enumerate((44, 64)):
+            for copy, m0, m1 in ((nc.scalar.copy, 0, split), (nc.vector.tensor_copy, split, P)):
+                pair = slice(2 * u, 2 * u + 2)
+                copy(
+                    grouped[2][:, pair, m0:m1, :].rearrange("p t m j -> p m j t"),
+                    raws[2][0][2][:].rearrange("p j (m t) -> p m j t", t=PACK)[:, m0:m1, :, pair],
+                )
         for t in range(PACK):
             quantize(2, t, t + 1)
             multiply(2, t)

@@ -18,7 +18,7 @@ MULT = mybir.AluOpType.mult
 P = 128
 PACK = 4
 TAPS = 3
-Y_SPLIT = 88
+Y_SPLIT = 72
 
 
 def tile_picked_gdconv_none_po_kernel(
@@ -156,32 +156,45 @@ def tile_picked_gdconv_none_po_kernel(
         y_scales = keep.tile([P, S], U8, name="y_scales", align_bytes=64)
         out_rows = out_0.rearrange("(p t) j -> p t j", t=PACK)
         words_out = out_1[0].rearrange("p c r -> p (c r)").bitcast(I32)
-        y = [keep.tile([P, PACK, H], F32, name="y%d" % h) for h in range(2)]
-        yb = [keep.tile([P, H, PACK], BF16, name="yb%d" % h, align_bytes=64) for h in range(2)]
+        y = keep.tile([P, PACK, S], F32, name="y")
+        yb = keep.tile([P, S, PACK], BF16, name="yb", align_bytes=64)
 
-        def views(h, c0, c1):
-            dst = yb[h][:, c0:c1, :].rearrange("p (c i) t -> p c t i", i=PACK)
-            return dst, y[h][:, :, c0:c1].rearrange("p t (c i) -> p c t i", i=PACK)
+        def product(t, c0, c1):
+            h = c0 // H
+            nc.vector.tensor_tensor(y[:, t, c0:c1], banks[t][:, c0:c1], gate[h][:, t, c0 - h * H : c1 - h * H], MULT)
 
-        def quantize_y(h):
-            cols = slice(h * H, (h + 1) * H)
-            nc.vector.quantize_mx(
-                out=y_words[:, cols].bitcast(FP8X4), scales=y_scales[:, cols], in_=yb[h][:].rearrange("p j t -> p (j t)")
+        def round_y(copy, c0, c1):
+            copy(
+                yb[:, c0:c1, :].rearrange("p (c i) t -> p c t i", i=PACK),
+                y[:, :, c0:c1].rearrange("p t (c i) -> p c t i", i=PACK),
             )
-            nc.sync.dma_start(words_out[:, cols], y_words[:, cols].bitcast(I32))
 
-        for h in range(2):
-            cols = slice(h * H, (h + 1) * H)
-            for t in range(PACK):
-                nc.vector.tensor_tensor(y[h][:, t, :], banks[t][:, cols], gate[h][:, t, :], MULT)
-                if t % 2:
-                    nc.sync.dma_start(out_rows[:, t - 1 : t + 1, cols], y[h][:, t - 1 : t + 1, :])
-            if h == 0:
-                nc.scalar.copy(*views(0, 0, H))
-        nc.scalar.copy(*views(1, 0, Y_SPLIT))
-        nc.vector.tensor_copy(*views(1, Y_SPLIT, H))
-        quantize_y(0)
-        quantize_y(1)
+        def quantize_y(c0, c1):
+            nc.vector.quantize_mx(
+                out=y_words[:, c0:c1].bitcast(FP8X4),
+                scales=y_scales[:, c0:c1],
+                in_=yb[:, c0:c1, :].rearrange("p j t -> p (j t)"),
+            )
+
+        Q = S // 4
+        for c0 in (0, H):
+            for t in range(2):
+                product(t, c0, c0 + H)
+        nc.sync.dma_start(out_rows[:, :2, :], y[:, :2, :])
+        for c0 in range(0, S, Q):
+            for t in range(2, PACK):
+                product(t, c0, c0 + Q)
+            if c0 < H:
+                round_y(nc.scalar.copy, c0, c0 + Q)
+        nc.sync.dma_start(out_rows[:, 2:, :], y[:, 2:, :])
+        round_y(nc.vector.tensor_copy, H, H + Q)
+        round_y(nc.scalar.copy, H + Q, H + Q + Y_SPLIT)
+        quantize_y(0, H)
+        nc.sync.dma_start(words_out[:, :H], y_words[:, :H].bitcast(I32))
+        round_y(nc.vector.tensor_copy, H + Q + Y_SPLIT, S)
+        quantize_y(H, H + Q)
+        quantize_y(H + Q, S)
+        nc.sync.dma_start(words_out[:, H:], y_words[:, H:].bitcast(I32))
         for q in range(4):
             eng = nc.scalar if q % 2 else nc.sync
             eng.dma_start(

@@ -177,16 +177,17 @@ def tile_picked_gdconv_none_po_kernel(
             )
 
         Q = S // 4
-        for c0 in (0, H):
-            for t in range(2):
+        for t in range(2):
+            for c0 in (0, H):
                 product(t, c0, c0 + H)
-        nc.sync.dma_start(out_rows[:, :2, :], y[:, :2, :])
+            nc.sync.dma_start(out_rows[:, t, :], y[:, t, :])
         for c0 in range(0, S, Q):
             for t in range(2, PACK):
                 product(t, c0, c0 + Q)
             if c0 < H:
                 round_y(nc.scalar.copy, c0, c0 + Q)
-        nc.sync.dma_start(out_rows[:, 2:, :], y[:, 2:, :])
+            if c0 % H:
+                nc.sync.dma_start(out_rows[:, 2:, c0 - Q : c0 + Q], y[:, 2:, c0 - Q : c0 + Q])
         round_y(nc.vector.tensor_copy, H, H + Q)
         round_y(nc.scalar.copy, H + Q, H + Q + Y_SPLIT)
         quantize_y(0, H)

@@ -134,9 +134,9 @@ def tile_picked_gdconv_none_po_kernel(
         gate = []
 
         def sigmoids(h):
-            gate.append(keep.tile([P, PACK, H], F32, name="gate%d" % h, tag=gate_tags[h], align_bytes=64))
-            for t in range(PACK):
-                nc.scalar.activation(gate[h][:, t, :], banks[PACK + t][:, h * H : (h + 1) * H], SIGMOID)
+            gate.append(keep.tile([P, 2, S], F32, name="gate%d" % h, tag=gate_tags[h], align_bytes=64))
+            for t in range(2):
+                nc.scalar.activation(gate[h][:, t, :], banks[PACK + 2 * h + t][:], SIGMOID)
 
         sigmoids(0)
         stage(1, 0)
@@ -160,8 +160,7 @@ def tile_picked_gdconv_none_po_kernel(
         yb = keep.tile([P, S, PACK], BF16, name="yb", align_bytes=64)
 
         def product(t, c0, c1):
-            h = c0 // H
-            nc.vector.tensor_tensor(y[:, t, c0:c1], banks[t][:, c0:c1], gate[h][:, t, c0 - h * H : c1 - h * H], MULT)
+            nc.vector.tensor_tensor(y[:, t, c0:c1], banks[t][:, c0:c1], gate[t // 2][:, t % 2, c0:c1], MULT)
 
         def round_y(copy, c0, c1):
             copy(
@@ -178,8 +177,7 @@ def tile_picked_gdconv_none_po_kernel(
 
         Q = S // 4
         for t in range(2):
-            for c0 in (0, H):
-                product(t, c0, c0 + H)
+            product(t, 0, S)
             nc.sync.dma_start(out_rows[:, t, :], y[:, t, :])
         for c0 in range(0, S, Q):
             for t in range(2, PACK):

@@ -123,11 +123,15 @@ def tile_picked_gdconv_none_po_kernel(
             for t in range(PACK):
                 multiply(i, t)
 
-        for t in range(PACK):
-            multiply(3, t)
-        stage(4, 128)
+        cast(4, 128)
+        quantize(4, 0, 4)
         load(2, "w5_then_w3")
-        stage(5, 64)
+        cast(5, 64)
+        quantize(5, 0, 4)
+        for t0 in (0, 2):
+            for i in (3, 4, 5):
+                for t in range(t0, t0 + 2):
+                    multiply(i, t)
         stage(0, 72)
         H = S // 2
         gate_tags = ("scale_table_then_w1", "w5_then_w3")
@@ -139,14 +143,23 @@ def tile_picked_gdconv_none_po_kernel(
                 nc.scalar.activation(gate[h][:, t, :], banks[PACK + 2 * h + t][:], SIGMOID)
 
         sigmoids(0)
-        stage(1, 0)
-        for u, split in enumerate((44, 64)):
-            for copy, m0, m1 in ((nc.scalar.copy, 0, split), (nc.vector.tensor_copy, split, P)):
-                pair = slice(2 * u, 2 * u + 2)
-                copy(
-                    grouped[2][:, pair, m0:m1, :].rearrange("p t m j -> p m j t"),
-                    raws[2][0][2][:].rearrange("p j (m t) -> p m j t", t=PACK)[:, m0:m1, :, pair],
-                )
+
+        def cast_by_pairs(i, splits):
+            for u, split in enumerate(splits):
+                for copy, m0, m1 in ((nc.scalar.copy, 0, split), (nc.vector.tensor_copy, split, P)):
+                    if m0 < m1:
+                        pair = slice(2 * u, 2 * u + 2)
+                        copy(
+                            grouped[i][:, pair, m0:m1, :].rearrange("p t m j -> p m j t"),
+                            raws[i][0][2][:].rearrange("p j (m t) -> p m j t", t=PACK)[:, m0:m1, :, pair],
+                        )
+
+        cast_by_pairs(1, (0, 56))
+        for t0 in (0, 2):
+            quantize(1, t0, t0 + 2)
+            for t in range(t0, t0 + 2):
+                multiply(1, t)
+        cast_by_pairs(2, (44, 64))
         for t in range(PACK):
             quantize(2, t, t + 1)
             multiply(2, t)

@@ -18,7 +18,6 @@ MULT = mybir.AluOpType.mult
 P = 128
 PACK = 4
 TAPS = 3
-Y_SPLIT = 72
 
 
 def tile_picked_gdconv_none_po_kernel(
@@ -134,15 +133,10 @@ def tile_picked_gdconv_none_po_kernel(
                     multiply(i, t)
         stage(0, 72)
         H = S // 2
-        gate_tags = ("scale_table_then_w1", "w5_then_w3")
-        gate = []
-
-        def sigmoids(h):
-            gate.append(keep.tile([P, 2, S], F32, name="gate%d" % h, tag=gate_tags[h], align_bytes=64))
-            for t in range(2):
-                nc.scalar.activation(gate[h][:, t, :], banks[PACK + 2 * h + t][:], SIGMOID)
-
-        sigmoids(0)
+        early = keep.tile([P, 3, S], F32, name="early", tag="scale_table_then_w1", align_bytes=64)
+        gate = [early[:, t, :] for t in range(3)]
+        for t in range(3):
+            nc.scalar.activation(gate[t], banks[PACK + t][:], SIGMOID)
 
         def cast_by_pairs(i, splits):
             for u, split in enumerate(splits):
@@ -154,16 +148,17 @@ def tile_picked_gdconv_none_po_kernel(
                             raws[i][0][2][:].rearrange("p j (m t) -> p m j t", t=PACK)[:, m0:m1, :, pair],
                         )
 
-        cast_by_pairs(1, (0, 56))
+        cast_by_pairs(1, (0, 0))
         for t0 in (0, 2):
             quantize(1, t0, t0 + 2)
             for t in range(t0, t0 + 2):
                 multiply(1, t)
         cast_by_pairs(2, (44, 64))
-        for t in range(PACK):
-            quantize(2, t, t + 1)
-            multiply(2, t)
-        sigmoids(1)
+
+        late = keep.tile([P, PACK - 3, S], F32, name="late", tag="w5_then_w3", align_bytes=64)
+        for t in range(3, PACK):
+            gate.append(late[:, t - 3, :])
+            nc.scalar.activation(gate[t], banks[PACK + t][:], SIGMOID)
 
         y_words = keep.tile([P, S], U32, name="y_words", align_bytes=64)
         y_scales = keep.tile([P, S], U8, name="y_scales", align_bytes=64)
@@ -173,7 +168,7 @@ def tile_picked_gdconv_none_po_kernel(
         yb = keep.tile([P, S, PACK], BF16, name="yb", align_bytes=64)
 
         def product(t, c0, c1):
-            nc.vector.tensor_tensor(y[:, t, c0:c1], banks[t][:, c0:c1], gate[t // 2][:, t % 2, c0:c1], MULT)
+            nc.vector.tensor_tensor(y[:, t, c0:c1], gate[t][:, c0:c1], banks[t][:, c0:c1], MULT)
 
         def round_y(copy, c0, c1):
             copy(
@@ -189,24 +184,33 @@ def tile_picked_gdconv_none_po_kernel(
             )
 
         Q = S // 4
-        for t in range(2):
-            product(t, 0, S)
-            nc.sync.dma_start(out_rows[:, t, :], y[:, t, :])
+        value = keep.tile([P, S], F32, name="value")
+        for t in range(PACK):
+            quantize(2, t, t + 1)
+            multiply(2, t)
+        for c0, c1 in zip((128, 288,), (288, 512,)):
+            nc.scalar.copy(value[:, c0:c1], banks[1][:, c0:c1])
+            nc.gpsimd.tensor_tensor(y[:, 1, c0:c1], value[:, c0:c1], gate[1][:, c0:c1], MULT)
+        product(0, 0, S)
+        nc.sync.dma_start(out_rows[:, 0, :], y[:, 0, :])
         for c0 in range(0, S, Q):
             for t in range(2, PACK):
                 product(t, c0, c0 + Q)
-            if c0 < H:
-                round_y(nc.scalar.copy, c0, c0 + Q)
+            if c0 == Q:
+                product(1, 0, Q)
             if c0 % H:
-                nc.sync.dma_start(out_rows[:, 2:, c0 - Q : c0 + Q], y[:, 2:, c0 - Q : c0 + Q])
-        round_y(nc.vector.tensor_copy, H, H + Q)
-        round_y(nc.scalar.copy, H + Q, H + Q + Y_SPLIT)
-        quantize_y(0, H)
-        nc.sync.dma_start(words_out[:, :H], y_words[:, :H].bitcast(I32))
-        round_y(nc.vector.tensor_copy, H + Q + Y_SPLIT, S)
-        quantize_y(H, H + Q)
+                nc.sync.dma_start(out_rows[:, 1:, c0 - Q : c0 + Q], y[:, 1:, c0 - Q : c0 + Q])
+            if c0 == Q:
+                round_y(nc.scalar.copy, 0, Q)
+                round_y(nc.scalar.copy, Q, 256)
+        round_y(nc.vector.tensor_copy, H + Q, S)
+        round_y(nc.vector.tensor_copy, 256, H + Q)
         quantize_y(H + Q, S)
+        quantize_y(0, Q)
+        quantize_y(H, H + Q)
         nc.sync.dma_start(words_out[:, H:], y_words[:, H:].bitcast(I32))
+        quantize_y(Q, H)
+        nc.sync.dma_start(words_out[:, :H], y_words[:, :H].bitcast(I32))
         for q in range(4):
             eng = nc.scalar if q % 2 else nc.sync
             eng.dma_start(

@@ -153,12 +153,6 @@ def tile_picked_gdconv_none_po_kernel(
             quantize(1, t0, t0 + 2)
             for t in range(t0, t0 + 2):
                 multiply(1, t)
-        cast_by_pairs(2, (44, 64))
-
-        late = keep.tile([P, PACK - 3, S], F32, name="late", tag="w5_then_w3", align_bytes=64)
-        for t in range(3, PACK):
-            gate.append(late[:, t - 3, :])
-            nc.scalar.activation(gate[t], banks[PACK + t][:], SIGMOID)
 
         y_words = keep.tile([P, S], U32, name="y_words", align_bytes=64)
         y_scales = keep.tile([P, S], U8, name="y_scales", align_bytes=64)
@@ -184,30 +178,51 @@ def tile_picked_gdconv_none_po_kernel(
             )
 
         Q = S // 4
-        value = keep.tile([P, S], F32, name="value")
-        for t in range(PACK):
+
+        def cast_pair(copy, u, m0, m1):
+            pair = slice(2 * u, 2 * u + 2)
+            copy(
+                grouped[2][:, pair, m0:m1, :].rearrange("p t m j -> p m j t"),
+                raws[2][0][2][:].rearrange("p j (m t) -> p m j t", t=PACK)[:, m0:m1, :, pair],
+            )
+
+        def close(t):
             quantize(2, t, t + 1)
             multiply(2, t)
-        for c0, c1 in zip((128, 288,), (288, 512,)):
-            nc.scalar.copy(value[:, c0:c1], banks[1][:, c0:c1])
-            nc.gpsimd.tensor_tensor(y[:, 1, c0:c1], value[:, c0:c1], gate[1][:, c0:c1], MULT)
+
+        cast_pair(nc.scalar.copy, 0, 0, 44)
+        cast_pair(nc.scalar.copy, 1, 0, 64)
+        cast_pair(nc.vector.tensor_copy, 0, 44, P)
+        cast_pair(nc.vector.tensor_copy, 1, 64, 96)
+        close(0)
+        cast_pair(nc.vector.tensor_copy, 1, 96, P)
+        late = keep.tile([P, S], F32, name="late", tag="w5_then_w3", align_bytes=64)
+        gate.append(late[:])
+        nc.scalar.activation(gate[3], banks[PACK + 3][:], SIGMOID)
+        close(1)
+        close(2)
+        close(3)
         product(0, 0, S)
         nc.sync.dma_start(out_rows[:, 0, :], y[:, 0, :])
+
+        value = keep.tile([P, 384], F32, name="value")
+        for c0, c1 in ((0, 160), (160, 384)):
+            nc.scalar.copy(value[:, c0:c1], banks[1][:, c0:c1])
+            nc.gpsimd.tensor_tensor(y[:, 1, c0:c1], value[:, c0:c1], gate[1][:, c0:c1], MULT)
+        product(2, 0, S)
+        nc.sync.dma_start(out_rows[:, 2, :], y[:, 2, :])
         for c0 in range(0, S, Q):
-            for t in range(2, PACK):
-                product(t, c0, c0 + Q)
-            if c0 == Q:
-                product(1, 0, Q)
-            if c0 % H:
-                nc.sync.dma_start(out_rows[:, 1:, c0 - Q : c0 + Q], y[:, 1:, c0 - Q : c0 + Q])
-            if c0 == Q:
-                round_y(nc.scalar.copy, 0, Q)
-                round_y(nc.scalar.copy, Q, 256)
+            product(3, c0, c0 + Q)
+            if c0 < H:
+                round_y(nc.scalar.copy, c0, c0 + Q)
+        nc.sync.dma_start(out_rows[:, 3, :], y[:, 3, :])
+        product(1, 384, S)
+        nc.sync.dma_start(out_rows[:, 1, :], y[:, 1, :])
+        round_y(nc.vector.tensor_copy, H, H + Q)
         round_y(nc.vector.tensor_copy, H + Q, S)
-        round_y(nc.vector.tensor_copy, 256, H + Q)
-        quantize_y(H + Q, S)
         quantize_y(0, Q)
         quantize_y(H, H + Q)
+        quantize_y(H + Q, S)
         nc.sync.dma_start(words_out[:, H:], y_words[:, H:].bitcast(I32))
         quantize_y(Q, H)
         nc.sync.dma_start(words_out[:, :H], y_words[:, :H].bitcast(I32))

@@ -28,10 +28,10 @@ def tile_picked_gdconv_none_po_kernel(
         keep = ctx.enter_context(tc.tile_pool(name="keep", bufs=1))
         psum = ctx.enter_context(tc.psum_pool(name="psum", bufs=1))
 
-        scale_table = keep.tile([P, T], U8, name="scale_table", tag="scale_table_then_w1", align_bytes=64)
+        scale_table = keep.tile([P, T], U8, name="scale_table", tag="scale_table_then_w1", align_bytes=256)
         nc.gpsimd.memset(scale_table[:, : T // 2].bitcast(I32), 0)
         nc.vector.memset(scale_table[:, T // 2 :].bitcast(I32), 0)
-        x_scale = keep.tile([P, TAPS * S], U8, name="x_scale", align_bytes=64)
+        x_scale = keep.tile([P, TAPS * S], U8, name="x_scale", align_bytes=256)
         nc.gpsimd.memset(x_scale[:].bitcast(I32), 0)
         warm = keep.tile([P, 2], F32, name="warm")
         nc.vector.memset(warm[:, 0:1], 0.0)
@@ -42,12 +42,12 @@ def tile_picked_gdconv_none_po_kernel(
         raws = {}
 
         def load(i, tag, m0=0, m1=P):
-            raw = keep.tile([P, PACK, PACK * (m1 - m0)], F32, name="raw%d_%d" % (i, m0), tag=tag, align_bytes=64)
+            raw = keep.tile([P, PACK, PACK * (m1 - m0)], F32, name="raw%d_%d" % (i, m0), tag=tag, align_bytes=256)
             rows = weights[i].rearrange("(p j) c -> p j c", j=PACK)
             nc.sync.dma_start(raw[:], rows[:, :, PACK * m0 : PACK * m1])
             raws.setdefault(i, []).append((m0, m1, raw))
 
-        word_table = keep.tile([P, T], I32, name="word_table", align_bytes=64)
+        word_table = keep.tile([P, T], I32, name="word_table", align_bytes=256)
         x_rows = x_words[0].rearrange("p c r -> p (c r)").bitcast(I32)
         nc.sync.dma_start(word_table[:, : T // 2], x_rows[:, : T // 2])
         for lst, src in zip(lists, (offs, tap1, tap2)):
@@ -84,7 +84,7 @@ def tile_picked_gdconv_none_po_kernel(
                 in_=grouped[i][:, t0:t1].rearrange("p t m j -> p (t m j)"),
             )
 
-        picked_scale = keep.tile([P, TAPS * S], U8, name="picked_scale", align_bytes=64)
+        picked_scale = keep.tile([P, TAPS * S], U8, name="picked_scale", align_bytes=256)
         x_tags = ("x_codes0", "x_codes1", "grouped3")
         x_codes = [keep.tile([P, S], U32, name="x_codes%d" % i, tag=x_tags[i], align_bytes=64) for i in range(TAPS)]
 
@@ -133,7 +133,7 @@ def tile_picked_gdconv_none_po_kernel(
                     multiply(i, t)
         stage(0, 72)
         H = S // 2
-        early = keep.tile([P, 3, S], F32, name="early", tag="scale_table_then_w1", align_bytes=64)
+        early = keep.tile([P, 3, S], F32, name="early", tag="scale_table_then_w1", align_bytes=256)
         gate = [early[:, t, :] for t in range(3)]
         for t in range(3):
             nc.scalar.activation(gate[t], banks[PACK + t][:], SIGMOID)
@@ -154,11 +154,11 @@ def tile_picked_gdconv_none_po_kernel(
             for t in range(t0, t0 + 2):
                 multiply(1, t)
 
-        y_words = keep.tile([P, S], U32, name="y_words", align_bytes=64)
-        y_scales = keep.tile([P, S], U8, name="y_scales", align_bytes=64)
+        y_words = keep.tile([P, S], U32, name="y_words", align_bytes=256)
+        y_scales = keep.tile([P, S], U8, name="y_scales", align_bytes=256)
         out_rows = out_0.rearrange("(p t) j -> p t j", t=PACK)
         words_out = out_1[0].rearrange("p c r -> p (c r)").bitcast(I32)
-        y = keep.tile([P, PACK, S], F32, name="y")
+        y = keep.tile([P, PACK, S], F32, name="y", align_bytes=256)
         yb = keep.tile([P, S, PACK], BF16, name="yb", align_bytes=64)
 
         def product(t, c0, c1):
@@ -196,7 +196,7 @@ def tile_picked_gdconv_none_po_kernel(
         cast_pair(nc.vector.tensor_copy, 1, 64, 96)
         close(0)
         cast_pair(nc.vector.tensor_copy, 1, 96, P)
-        late = keep.tile([P, S], F32, name="late", tag="w5_then_w3", align_bytes=64)
+        late = keep.tile([P, S], F32, name="late", tag="w5_then_w3", align_bytes=256)
         gate.append(late[:])
         nc.scalar.activation(gate[3], banks[PACK + 3][:], SIGMOID)
         close(1)

@@ -227,7 +227,6 @@ def tile_picked_gdconv_none_po_kernel(
         quantize_y(Q, H)
         nc.sync.dma_start(words_out[:, :H], y_words[:, :H].bitcast(I32))
         for q in range(4):
-            eng = nc.scalar if q % 2 else nc.sync
-            eng.dma_start(
+            nc.sync.dma_start(
                 out_2[0, 4 * q : 4 * q + 4, :].bitcast(I32), y_scales[32 * q : 32 * q + 4, :].bitcast(I32)
             )

@@ -127,15 +127,15 @@ def tile_picked_gdconv_none_po_kernel(
         load(2, "w5_then_w3")
         cast(5, 64)
         quantize(5, 0, 4)
-        for t0 in (0, 2):
+        for pair in ((0, 1), (3, 2)):
             for i in (3, 4, 5):
-                for t in range(t0, t0 + 2):
+                for t in pair:
                     multiply(i, t)
         stage(0, 72)
         H = S // 2
         early = keep.tile([P, 3, S], F32, name="early", tag="scale_table_then_w1", align_bytes=256)
-        gate = [early[:, t, :] for t in range(3)]
-        for t in range(3):
+        gate = {t: early[:, slot, :] for slot, t in enumerate((0, 1, 3))}
+        for t in gate:
             nc.scalar.activation(gate[t], banks[PACK + t][:], SIGMOID)
 
         def cast_by_pairs(i, splits):
@@ -197,11 +197,11 @@ def tile_picked_gdconv_none_po_kernel(
         close(0)
         cast_pair(nc.vector.tensor_copy, 1, 96, P)
         late = keep.tile([P, S], F32, name="late", tag="w5_then_w3", align_bytes=256)
-        gate.append(late[:])
-        nc.scalar.activation(gate[3], banks[PACK + 3][:], SIGMOID)
+        gate[2] = late[:]
+        nc.scalar.activation(gate[2], banks[PACK + 2][:], SIGMOID)
         close(1)
-        close(2)
         close(3)
+        close(2)
         product(0, 0, S)
         nc.sync.dma_start(out_rows[:, 0, :], y[:, 0, :])
 
@@ -209,15 +209,14 @@ def tile_picked_gdconv_none_po_kernel(
         for c0, c1 in ((0, 160), (160, 384)):
             nc.scalar.copy(value[:, c0:c1], banks[1][:, c0:c1])
             nc.gpsimd.tensor_tensor(y[:, 1, c0:c1], value[:, c0:c1], gate[1][:, c0:c1], MULT)
-        product(2, 0, S)
-        nc.sync.dma_start(out_rows[:, 2, :], y[:, 2, :])
+        product(3, 0, S)
+        nc.sync.dma_start(out_rows[:, 3, :], y[:, 3, :])
         for c0 in range(0, S, Q):
-            product(3, c0, c0 + Q)
+            product(2, c0, c0 + Q)
             if c0 < H:
                 round_y(nc.scalar.copy, c0, c0 + Q)
-        nc.sync.dma_start(out_rows[:, 3, :], y[:, 3, :])
         product(1, 384, S)
-        nc.sync.dma_start(out_rows[:, 1, :], y[:, 1, :])
+        nc.sync.dma_start(out_rows[:, 1:3, :], y[:, 1:3, :])
         round_y(nc.vector.tensor_copy, H, H + Q)
         round_y(nc.vector.tensor_copy, H + Q, S)
         quantize_y(0, Q)

@@ -226,6 +226,7 @@ def tile_picked_gdconv_none_po_kernel(
         quantize_y(Q, H)
         nc.sync.dma_start(words_out[:, :H], y_words[:, :H].bitcast(I32))
         for q in range(4):
-            nc.sync.dma_start(
+            eng = nc.scalar if q % 2 else nc.sync
+            eng.dma_start(
                 out_2[0, 4 * q : 4 * q + 4, :].bitcast(I32), y_scales[32 * q : 32 * q + 4, :].bitcast(I32)
             )

from contextlib import ExitStack

import concourse.mybir as mybir

K, T, S, N = 512, 2048, 512, 512
FLOPS = 2 * 6 * K * N * S

F32 = mybir.dt.float32
BF16 = mybir.dt.bfloat16
I32 = mybir.dt.int32
U32 = mybir.dt.uint32
U16 = mybir.dt.uint16
U8 = mybir.dt.uint8
FP8X4 = mybir.dt.float8_e4m3fn_x4
SIGMOID = mybir.ActivationFunctionType.Sigmoid
MULT = mybir.AluOpType.mult

P = 128
PACK = 4
TAPS = 3


def tile_picked_gdconv_none_po_kernel(
    tc, x_words, x_scales, w1, w2, w3, w4, w5, w6, offs, tap1, tap2, out_0, out_1, out_2
):
    nc = tc.nc
    with ExitStack() as ctx:
        keep = ctx.enter_context(tc.tile_pool(name="keep", bufs=1))
        psum = ctx.enter_context(tc.psum_pool(name="psum", bufs=1))

        scale_table = keep.tile([P, T], U8, name="scale_table", tag="scale_table_then_w1", align_bytes=256)
        nc.gpsimd.memset(scale_table[:, : T // 2].bitcast(I32), 0)
        nc.vector.memset(scale_table[:, T // 2 :].bitcast(I32), 0)
        x_scale = keep.tile([P, TAPS * S], U8, name="x_scale", align_bytes=256)
        nc.gpsimd.memset(x_scale[:].bitcast(I32), 0)
        warm = keep.tile([P, 2], F32, name="warm")
        nc.vector.memset(warm[:, 0:1], 0.0)
        nc.scalar.activation(warm[:, 1:2], warm[:, 0:1], SIGMOID)

        lists = [keep.tile([P, S // 16], U16, name="list%d" % i) for i in range(TAPS)]
        weights = (w1, w2, w3, w4, w5, w6)
        raws = {}

        def load(i, tag, m0=0, m1=P):
            raw = keep.tile([P, PACK, PACK * (m1 - m0)], F32, name="raw%d_%d" % (i, m0), tag=tag, align_bytes=256)
            rows = weights[i].rearrange("(p j) c -> p j c", j=PACK)
            nc.sync.dma_start(raw[:], rows[:, :, PACK * m0 : PACK * m1])
            raws.setdefault(i, []).append((m0, m1, raw))

        word_table = keep.tile([P, T], I32, name="word_table", align_bytes=256)
        x_rows = x_words[0].rearrange("p c r -> p (c r)").bitcast(I32)
        nc.sync.dma_start(word_table[:, : T // 2], x_rows[:, : T // 2])
        for lst, src in zip(lists, (offs, tap1, tap2)):
            nc.sync.dma_start(lst[:], src)
        nc.sync.dma_start(scale_table[0:P:8, :].bitcast(I32), x_scales[0].bitcast(I32))
        load(3, "w4_then_w2")
        nc.sync.dma_start(word_table[:, T // 2 :], x_rows[:, T // 2 :])
        load(4, "w5_then_w3")
        load(5, "w6")

        grouped = [
            keep.tile([P, PACK, P, PACK], BF16, name="grouped%d" % i, tag="grouped%d" % i, align_bytes=64)
            for i in range(6)
        ]
        codes = [keep.tile([P, N], U32, name="codes%d" % i, align_bytes=64) for i in range(6)]
        scales = [keep.tile([P, N], U8, name="scales%d" % i, align_bytes=64) for i in range(6)]

        def cast(i, split, first=0, last=P):
            for engine, m0, m1 in (("scalar", first, split), ("vector", split, last)):
                if m0 == m1:
                    continue
                dst = grouped[i][:, :, m0:m1, :].rearrange("p t m j -> p m j t")
                base, raw = [(a, r) for a, b, r in raws[i] if a <= m0 and m1 <= b][0]
                src = raw[:, :, PACK * (m0 - base) : PACK * (m1 - base)].rearrange("p j (m t) -> p m j t", t=PACK)
                if engine == "scalar":
                    nc.scalar.copy(dst, src)
                else:
                    nc.vector.tensor_copy(dst, src)

        def quantize(i, t0, t1):
            nc.vector.quantize_mx(
                out=codes[i][:, t0 * P : t1 * P].bitcast(FP8X4),
                scales=scales[i][:, t0 * P : t1 * P],
                in_=grouped[i][:, t0:t1].rearrange("p t m j -> p (t m j)"),
            )

        picked_scale = keep.tile([P, TAPS * S], U8, name="picked_scale", align_bytes=256)
        x_tags = ("x_codes0", "x_codes1", "grouped3")
        x_codes = [keep.tile([P, S], U32, name="x_codes%d" % i, tag=x_tags[i], align_bytes=64) for i in range(TAPS)]

        for i in range(TAPS):
            nc.vector.tensor_copy(picked_scale[:, i * S : (i + 1) * S], scale_table[:].indirect(lists[i][:]))
        for q in range(4):
            nc.sync.dma_start(
                x_scale[32 * q : 32 * q + 4, :].bitcast(I32), picked_scale[32 * q : 32 * q + 32 : 8, :].bitcast(I32)
            )
        load(0, "scale_table_then_w1")
        cast(3, 128)
        load(1, "w4_then_w2")
        for i in range(TAPS):
            if i == 2:
                quantize(3, 0, 4)
            nc.vector.tensor_copy(x_codes[i][:], word_table[:].bitcast(U32).indirect(lists[i][:]))

        banks = [psum.tile([P, S], F32, name="bank%d" % b) for b in range(8)]

        def multiply(i, t):
            tap = i % TAPS
            nc.tensor.matmul_mx(
                out=banks[(i // TAPS) * PACK + t][:],
                lhsT=codes[i][:, t * P : (t + 1) * P].bitcast(FP8X4),
                lhsT_scale=scales[i][:, t * P : (t + 1) * P],
                rhs=x_codes[tap][:].bitcast(FP8X4),
                rhs_scale=x_scale[:, tap * S : (tap + 1) * S],
                start=(tap == 0),
                stop=(tap == TAPS - 1),
            )

        def stage(i, split):
            cast(i, split)
            quantize(i, 0, 4)
            for t in range(PACK):
                multiply(i, t)

        cast(4, 128)
        quantize(4, 0, 4)
        load(2, "w5_then_w3")
        cast(5, 64)
        quantize(5, 0, 4)
        for pair in ((0, 1), (3, 2)):
            for i in (3, 4, 5):
                for t in pair:
                    multiply(i, t)
        stage(0, 72)
        H = S // 2
        early = keep.tile([P, 3, S], F32, name="early", tag="scale_table_then_w1", align_bytes=256)
        gate = {t: early[:, slot, :] for slot, t in enumerate((0, 1, 3))}
        for t in gate:
            nc.scalar.activation(gate[t], banks[PACK + t][:], SIGMOID)

        def cast_by_pairs(i, splits):
            for u, split in enumerate(splits):
                for copy, m0, m1 in ((nc.scalar.copy, 0, split), (nc.vector.tensor_copy, split, P)):
                    if m0 < m1:
                        pair = slice(2 * u, 2 * u + 2)
                        copy(
                            grouped[i][:, pair, m0:m1, :].rearrange("p t m j -> p m j t"),
                            raws[i][0][2][:].rearrange("p j (m t) -> p m j t", t=PACK)[:, m0:m1, :, pair],
                        )

        cast_by_pairs(1, (0, 0))
        for t0 in (0, 2):
            quantize(1, t0, t0 + 2)
            for t in range(t0, t0 + 2):
                multiply(1, t)

        y_words = keep.tile([P, S], U32, name="y_words", align_bytes=256)
        y_scales = keep.tile([P, S], U8, name="y_scales", align_bytes=256)
        out_rows = out_0.rearrange("(p t) j -> p t j", t=PACK)
        words_out = out_1[0].rearrange("p c r -> p (c r)").bitcast(I32)
        y = keep.tile([P, PACK, S], F32, name="y", align_bytes=256)
        yb = keep.tile([P, S, PACK], BF16, name="yb", align_bytes=64)

        def product(t, c0, c1):
            nc.vector.tensor_tensor(y[:, t, c0:c1], gate[t][:, c0:c1], banks[t][:, c0:c1], MULT)

        def round_y(copy, c0, c1):
            copy(
                yb[:, c0:c1, :].rearrange("p (c i) t -> p c t i", i=PACK),
                y[:, :, c0:c1].rearrange("p t (c i) -> p c t i", i=PACK),
            )

        def quantize_y(c0, c1):
            nc.vector.quantize_mx(
                out=y_words[:, c0:c1].bitcast(FP8X4),
                scales=y_scales[:, c0:c1],
                in_=yb[:, c0:c1, :].rearrange("p j t -> p (j t)"),
            )

        Q = S // 4

        def cast_pair(copy, u, m0, m1):
            pair = slice(2 * u, 2 * u + 2)
            copy(
                grouped[2][:, pair, m0:m1, :].rearrange("p t m j -> p m j t"),
                raws[2][0][2][:].rearrange("p j (m t) -> p m j t", t=PACK)[:, m0:m1, :, pair],
            )

        def close(t):
            quantize(2, t, t + 1)
            multiply(2, t)

        cast_pair(nc.scalar.copy, 0, 0, 44)
        cast_pair(nc.scalar.copy, 1, 0, 64)
        cast_pair(nc.vector.tensor_copy, 0, 44, P)
        cast_pair(nc.vector.tensor_copy, 1, 64, 96)
        close(0)
        cast_pair(nc.vector.tensor_copy, 1, 96, P)
        late = keep.tile([P, S], F32, name="late", tag="w5_then_w3", align_bytes=256)
        gate[2] = late[:]
        nc.scalar.activation(gate[2], banks[PACK + 2][:], SIGMOID)
        close(1)
        close(3)
        close(2)
        product(0, 0, S)
        nc.sync.dma_start(out_rows[:, 0, :], y[:, 0, :])

        value = keep.tile([P, 384], F32, name="value")
        for c0, c1 in ((0, 160), (160, 384)):
            nc.scalar.copy(value[:, c0:c1], banks[1][:, c0:c1])
            nc.gpsimd.tensor_tensor(y[:, 1, c0:c1], value[:, c0:c1], gate[1][:, c0:c1], MULT)
        product(3, 0, S)
        nc.sync.dma_start(out_rows[:, 3, :], y[:, 3, :])
        for c0 in range(0, S, Q):
            product(2, c0, c0 + Q)
            if c0 < H:
                round_y(nc.scalar.copy, c0, c0 + Q)
        product(1, 384, S)
        nc.sync.dma_start(out_rows[:, 1:3, :], y[:, 1:3, :])
        round_y(nc.vector.tensor_copy, H, H + Q)
        round_y(nc.vector.tensor_copy, H + Q, S)
        quantize_y(0, Q)
        quantize_y(H, H + Q)
        quantize_y(H + Q, S)
        nc.sync.dma_start(words_out[:, H:], y_words[:, H:].bitcast(I32))
        quantize_y(Q, H)
        nc.sync.dma_start(words_out[:, :H], y_words[:, :H].bitcast(I32))
        for q in range(4):
            eng = nc.scalar if q % 2 else nc.sync
            eng.dma_start(
                out_2[0, 4 * q : 4 * q + 4, :].bitcast(I32), y_scales[32 * q : 32 * q + 4, :].bitcast(I32)
            )
